import numpy as np
import ml_dtypes

BF16 = ml_dtypes.bfloat16


def bf(x):
    return np.asarray(x, np.float32).astype(BF16)


def f32(x):
    return np.asarray(x, np.float32)


def f64(x):
    return np.asarray(x).astype(np.float64)


def striped(idx):
    return np.concatenate([l.reshape(-1, 16).T for l in idx])


def rows(idx, k):
    return np.tile(np.repeat(idx, 16, axis=0), (k // (16 * 8), 1))


def look(tab, idx):
    return np.take_along_axis(f64(tab), rows(idx, len(tab)), axis=1)


K, S, D, V, N, M = 256, 2048, 2, 512, 1024, 256


def setup_inputs():
    return {"tab": f32(np.random.standard_normal((K, S))), "x0": f32(1.0 * np.random.standard_normal((K, V))), "w": bf(np.random.standard_normal((K, M)) / np.sqrt(K)), "b": f32(0.5 * np.random.standard_normal((M, 1))), "offs": striped(np.stack([np.random.permutation(S)[:N] for _ in range(8)]))}


def reference(tab, x0, w, b, offs):
    idx = np.stack([g.T.reshape(-1) for g in np.split(offs, 8)])
    hi = lo = f64(x0)
    for d in range(D):
        hi, lo = np.maximum(hi, look(tab, idx[:, d * V:(d + 1) * V])), np.minimum(lo, look(tab, idx[:, d * V:(d + 1) * V]))
    x = hi - lo
    return np.maximum(f64(w).T @ x + f64(b), 0.0)

@@ -1,0 +1,70 @@
+import concourse.mybir as mybir
+
+F32, BF16, U16 = mybir.dt.float32, mybir.dt.bfloat16, mybir.dt.uint16
+MAX, MIN = mybir.AluOpType.max, mybir.AluOpType.min
+ADD, SUBTRACT = mybir.AluOpType.add, mybir.AluOpType.subtract
+RELU = mybir.ActivationFunctionType.Relu
+
+P = 128
+K, S = 256, 2048
+D, V = 2, 512
+M = 256
+FLOPS = 2 * K * M * V
+
+
+def tile_lookup_span_relu_kernel(tc, tab, x0, w, b, offs, out):
+    nc = tc.nc
+    row_blocks, out_blocks = K // P, M // P
+    list_cols = V // 16
+
+    with (
+        tc.tile_pool(name="held", bufs=1) as held,
+        tc.psum_pool(name="psum", bufs=1) as psum,
+    ):
+        offsets = held.tile([P, D * list_cols], U16, name="offsets")
+        nc.sync.dma_start(offsets[:], offs)
+
+        windows, own = [], []
+        for r in range(row_blocks):
+            rows = slice(r * P, (r + 1) * P)
+            own_r = held.tile([P, V], F32, name=f"own{r}")
+            nc.scalar.dma_start(own_r[:], x0[rows, :])
+            window_r = held.tile([P, S], F32, name=f"window{r}")
+            nc.sync.dma_start(window_r[:], tab[rows, :])
+            own.append(own_r)
+            windows.append(window_r)
+
+        weights = held.tile([P, row_blocks, M], BF16, name="weights")
+        nc.scalar.dma_start(weights[:], w.rearrange("(r p) m -> p r m", p=P))
+        bias = held.tile([P, out_blocks], F32, name="bias")
+        nc.scalar.dma_start(bias[:], b.rearrange("(m p) o -> p (m o)", p=P))
+
+        sums = [psum.tile([P, V], F32, name=f"sums{m}") for m in range(out_blocks)]
+        for r in range(row_blocks):
+            highest = lowest = own[r]
+            for d in range(D):
+                neighbour = windows[r][:].indirect(offsets[:, d * list_cols : (d + 1) * list_cols])
+                higher = held.tile([P, V], F32, name=f"higher{r}_{d}")
+                nc.vector.tensor_tensor(higher[:], neighbour, highest[:], MAX)
+                lower = held.tile([P, V], F32, name=f"lower{r}_{d}")
+                nc.vector.tensor_tensor(lower[:], neighbour, lowest[:], MIN)
+                highest, lowest = higher, lower
+            span = held.tile([P, V], BF16, name=f"span{r}")
+            nc.vector.tensor_tensor(span[:], highest[:], lowest[:], SUBTRACT)
+            for m in range(out_blocks):
+                nc.tensor.matmul(
+                    sums[m][:],
+                    weights[:, r, m * P : (m + 1) * P],
+                    span[:],
+                    start=(r == 0),
+                    stop=(r == row_blocks - 1),
+                )
+
+        for m in range(out_blocks):
+            result = held.tile([P, V], F32, name=f"result{m}")
+            if m % 2 == 0:
+                nc.scalar.activation(result[:], sums[m][:], RELU, bias=bias[:, m : m + 1])
+                nc.scalar.dma_start(out[m * P : (m + 1) * P, :], result[:])
+            else:
+                nc.vector.tensor_scalar(result[:], sums[m][:], bias[:, m : m + 1], 0.0, ADD, MAX)
+                nc.sync.dma_start(out[m * P : (m + 1) * P, :], result[:])

@@ -1,4 +1,5 @@
 import concourse.mybir as mybir
+from concourse.masks import make_identity
 
 F32, BF16, U16 = mybir.dt.float32, mybir.dt.bfloat16, mybir.dt.uint16
 MAX, MIN = mybir.AluOpType.max, mybir.AluOpType.min
@@ -9,6 +10,7 @@ P = 128
 K, S = 256, 2048
 D, V = 2, 512
 M = 256
+H = V // 2
 FLOPS = 2 * K * M * V
 
 
@@ -39,7 +41,13 @@ def tile_lookup_span_relu_kernel(tc, tab, x0, w, b, offs, out):
         bias = held.tile([P, out_blocks], F32, name="bias")
         nc.scalar.dma_start(bias[:], b.rearrange("(m p) o -> p (m o)", p=P))
 
-        sums = [psum.tile([P, V], F32, name=f"sums{m}") for m in range(out_blocks)]
+        plus = held.tile([P, P], F32, name="plus")
+        make_identity(nc, plus[:])
+        minus = held.tile([P, P], F32, name="minus")
+        nc.scalar.mul(minus[:], plus[:], -1.0)
+
+        halves = [slice(h, h + H) for h in range(0, V, H)]
+        sums = [[psum.tile([P, H], F32, name=f"sums{m}_{h}") for h in range(len(halves))] for m in range(out_blocks)]
         for r in range(row_blocks):
             highest = lowest = own[r]
             for d in range(D):
@@ -49,22 +57,32 @@ def tile_lookup_span_relu_kernel(tc, tab, x0, w, b, offs, out):
                 lower = held.tile([P, V], F32, name=f"lower{r}_{d}")
                 nc.vector.tensor_tensor(lower[:], neighbour, lowest[:], MIN)
                 highest, lowest = higher, lower
-            span = held.tile([P, V], BF16, name=f"span{r}")
-            nc.vector.tensor_tensor(span[:], highest[:], lowest[:], SUBTRACT)
-            for m in range(out_blocks):
-                nc.tensor.matmul(
-                    sums[m][:],
-                    weights[:, r, m * P : (m + 1) * P],
-                    span[:],
-                    start=(r == 0),
-                    stop=(r == row_blocks - 1),
-                )
+            last = r == row_blocks - 1
+            if not last:
+                difference = psum.tile([P, V], F32, name=f"difference{r}")
+                nc.tensor.matmul(difference[:], plus[:], highest[:], start=True, stop=False)
+                nc.tensor.matmul(difference[:], minus[:], lowest[:], start=False, stop=True)
+            for h, cols in enumerate(halves):
+                span = held.tile([P, H], BF16, name=f"span{r}_{h}")
+                if last:
+                    nc.vector.tensor_tensor(span[:], highest[:, cols], lowest[:, cols], SUBTRACT)
+                else:
+                    nc.scalar.copy(span[:], difference[:, cols])
+                for m in range(out_blocks):
+                    nc.tensor.matmul(
+                        sums[m][h][:],
+                        weights[:, r, m * P : (m + 1) * P],
+                        span[:],
+                        start=(r == 0),
+                        stop=last,
+                    )
 
-        for m in range(out_blocks):
-            result = held.tile([P, V], F32, name=f"result{m}")
-            if m % 2 == 0:
-                nc.scalar.activation(result[:], sums[m][:], RELU, bias=bias[:, m : m + 1])
-                nc.scalar.dma_start(out[m * P : (m + 1) * P, :], result[:])
-            else:
-                nc.vector.tensor_scalar(result[:], sums[m][:], bias[:, m : m + 1], 0.0, ADD, MAX)
-                nc.sync.dma_start(out[m * P : (m + 1) * P, :], result[:])
+        for h, cols in enumerate(halves):
+            for m in range(out_blocks):
+                result = held.tile([P, H], F32, name=f"result{m}_{h}")
+                if m % 2 == 0:
+                    nc.scalar.activation(result[:], sums[m][h][:], RELU, bias=bias[:, m : m + 1])
+                    nc.scalar.dma_start(out[m * P : (m + 1) * P, cols], result[:])
+                else:
+                    nc.vector.tensor_scalar(result[:], sums[m][h][:], bias[:, m : m + 1], 0.0, ADD, MAX)
+                    nc.sync.dma_start(out[m * P : (m + 1) * P, cols], result[:])

@@ -32,7 +32,8 @@ def tile_lookup_span_relu_kernel(tc, tab, x0, w, b, offs, out):
             own_r = held.tile([P, V], F32, name=f"own{r}")
             nc.scalar.dma_start(own_r[:], x0[rows, :])
             window_r = held.tile([P, S], F32, name=f"window{r}")
-            nc.sync.dma_start(window_r[:], tab[rows, :])
+            nc.sync.dma_start(window_r[:, : S // 2], tab[rows, : S // 2])
+            nc.scalar.dma_start(window_r[:, S // 2 :], tab[rows, S // 2 :])
             own.append(own_r)
             windows.append(window_r)
 

import concourse.mybir as mybir
from concourse.masks import make_identity

F32, BF16, U16 = mybir.dt.float32, mybir.dt.bfloat16, mybir.dt.uint16
MAX, MIN = mybir.AluOpType.max, mybir.AluOpType.min
ADD, SUBTRACT = mybir.AluOpType.add, mybir.AluOpType.subtract
RELU = mybir.ActivationFunctionType.Relu

P = 128
K, S = 256, 2048
D, V = 2, 512
M = 256
H = V // 2
FLOPS = 2 * K * M * V


def tile_lookup_span_relu_kernel(tc, tab, x0, w, b, offs, out):
    nc = tc.nc
    row_blocks, out_blocks = K // P, M // P
    list_cols = V // 16

    with (
        tc.tile_pool(name="held", bufs=1) as held,
        tc.psum_pool(name="psum", bufs=1) as psum,
    ):
        offsets = held.tile([P, D * list_cols], U16, name="offsets")
        nc.sync.dma_start(offsets[:], offs)

        windows, own = [], []
        for r in range(row_blocks):
            rows = slice(r * P, (r + 1) * P)
            own_r = held.tile([P, V], F32, name=f"own{r}")
            nc.scalar.dma_start(own_r[:], x0[rows, :])
            window_r = held.tile([P, S], F32, name=f"window{r}")
            nc.sync.dma_start(window_r[:, : S // 2], tab[rows, : S // 2])
            nc.scalar.dma_start(window_r[:, S // 2 :], tab[rows, S // 2 :])
            own.append(own_r)
            windows.append(window_r)

        weights = held.tile([P, row_blocks, M], BF16, name="weights")
        nc.scalar.dma_start(weights[:], w.rearrange("(r p) m -> p r m", p=P))
        bias = held.tile([P, out_blocks], F32, name="bias")
        nc.scalar.dma_start(bias[:], b.rearrange("(m p) o -> p (m o)", p=P))

        plus = held.tile([P, P], F32, name="plus")
        make_identity(nc, plus[:])
        minus = held.tile([P, P], F32, name="minus")
        nc.scalar.mul(minus[:], plus[:], -1.0)

        halves = [slice(h, h + H) for h in range(0, V, H)]
        sums = [[psum.tile([P, H], F32, name=f"sums{m}_{h}") for h in range(len(halves))] for m in range(out_blocks)]
        for r in range(row_blocks):
            highest = lowest = own[r]
            for d in range(D):
                neighbour = windows[r][:].indirect(offsets[:, d * list_cols : (d + 1) * list_cols])
                higher = held.tile([P, V], F32, name=f"higher{r}_{d}")
                nc.vector.tensor_tensor(higher[:], neighbour, highest[:], MAX)
                lower = held.tile([P, V], F32, name=f"lower{r}_{d}")
                nc.vector.tensor_tensor(lower[:], neighbour, lowest[:], MIN)
                highest, lowest = higher, lower
            last = r == row_blocks - 1
            if not last:
                difference = psum.tile([P, V], F32, name=f"difference{r}")
                nc.tensor.matmul(difference[:], plus[:], highest[:], start=True, stop=False)
                nc.tensor.matmul(difference[:], minus[:], lowest[:], start=False, stop=True)
            for h, cols in enumerate(halves):
                span = held.tile([P, H], BF16, name=f"span{r}_{h}")
                if last:
                    nc.vector.tensor_tensor(span[:], highest[:, cols], lowest[:, cols], SUBTRACT)
                else:
                    nc.scalar.copy(span[:], difference[:, cols])
                for m in range(out_blocks):
                    nc.tensor.matmul(
                        sums[m][h][:],
                        weights[:, r, m * P : (m + 1) * P],
                        span[:],
                        start=(r == 0),
                        stop=last,
                    )

        for h, cols in enumerate(halves):
            for m in range(out_blocks):
                result = held.tile([P, H], F32, name=f"result{m}_{h}")
                if m % 2 == 0:
                    nc.scalar.activation(result[:], sums[m][h][:], RELU, bias=bias[:, m : m + 1])
                    nc.scalar.dma_start(out[m * P : (m + 1) * P, cols], result[:])
                else:
                    nc.vector.tensor_scalar(result[:], sums[m][h][:], bias[:, m : m + 1], 0.0, ADD, MAX)
                    nc.sync.dma_start(out[m * P : (m + 1) * P, cols], result[:])
